import numpy as np
import ml_dtypes


def mxq(x, axis, fmt="e4m3"):
    dtype, down = {"e4m3": (ml_dtypes.float8_e4m3fn, 7), "e5m2": (ml_dtypes.float8_e5m2, 14)}[fmt]
    v = np.moveaxis(np.asarray(x, np.float32).astype(ml_dtypes.bfloat16).astype(np.float64), axis, -1)
    blocks = v.reshape(v.shape[:-1] + (-1, 32))
    amax = np.abs(blocks).max(-1, keepdims=True)
    byte = np.maximum(np.where(amax > 0, np.frexp(amax)[1] - 1 + 127, 0) - down, 1)
    scale = np.exp2(byte - 127.0)
    codes = (blocks / scale).astype(np.float32).astype(dtype).astype(np.float64)
    return np.moveaxis((codes * scale).reshape(v.shape), -1, axis)


WIDE = False


def mx_kscale(k):
    if not WIDE:
        return np.ones(k)
    levels = np.array([10, -10, 5, -5, 0])
    if k % 512:
        return np.exp2(np.random.permutation(np.resize(levels, k // 32))).repeat(32)
    a = np.empty((k // 512, 16))
    for p in range(k // 512):
        a[p, :8] = np.random.permutation(np.resize(levels, 8))
        for g in range(8):
            far = levels[np.abs(levels - a[p, g]) >= 10]
            a[p, g + 8] = far[np.random.randint(len(far))]
    return np.exp2(a.ravel()).repeat(32)


def f64(x):
    return np.asarray(x).astype(np.float64)


def striped(idx):
    return np.tile(idx.reshape(-1, 16).T, (8, 1)).astype(np.uint16)


def unstriped(offs):
    return offs[:16].T.reshape(-1).astype(np.int64)


def striped8(idx):
    return np.concatenate([x.reshape(-1, 16).T for x in idx]).astype(np.uint16)


def runs(offs, k):
    lists = np.stack([offs[16 * r : 16 * r + 16].T.reshape(-1) for r in range(8)]).astype(np.int64)
    return lists[np.arange(k) % 512 // 64]


def pack_weight(w):
    k, n = w.shape
    w = f64(np.asarray(w, np.float32).astype(ml_dtypes.bfloat16)).reshape(k // 32, 32, n)
    amax = np.abs(w).max(1)
    byte = np.clip(np.where(amax > 0, np.frexp(amax)[1] - 1 + 127 - 7, 1), 1, 254)
    scaled = (w * np.exp2(127.0 - byte)[:, None, :]).reshape(k, n).astype(np.float32)
    words = np.ascontiguousarray(scaled.reshape(k // 512, 128, 4, n).transpose(0, 1, 3, 2)).astype(ml_dtypes.float8_e4m3fn).view(np.uint8)
    return words, np.ascontiguousarray(byte.astype(np.uint8).reshape(k // 512, 16, n))


def unpack_weight(words, scales):
    g, p, n, _ = words.shape
    vals = np.ascontiguousarray(words).view(ml_dtypes.float8_e4m3fn).astype(np.float64) * np.repeat(np.exp2(scales.astype(np.float64) - 127.0), 8, axis=1)[..., None]
    return vals.transpose(0, 1, 3, 2).reshape(g * 512, n)


def sigmoid(v):
    return 1.0 / (1.0 + np.exp(-np.maximum(v, -700.0)))


K, T, S, N, G, H, U = 512, 1024, 256, 512, 2048, 512, 512


def setup_inputs():
    n = np.random.standard_normal
    s = mx_kscale(K)[:, None]
    u = mx_kscale(K)
    packed_xT = pack_weight(n((K, T)) * s)
    packed_dT = pack_weight(n((K, G)) / s)
    perm = np.random.permutation(U)
    return {
        "x_words": packed_xT[0],
        "x_scales": packed_xT[1],
        "d_words": packed_dT[0],
        "d_scales": packed_dT[1],
        "sl": np.random.uniform(1.0, 2.0, (H, 1)).astype(np.float32),
        "th": (0.5 * n((H, 1))).astype(np.float32),
        "gn": (np.random.uniform(0.5, 1.5, (H, 1)) * u[:, None]).astype(np.float32),
        "w1": (n((H, N)) / np.sqrt(H) / u[:, None]).astype(np.float32),
        "offs": striped(np.random.permutation(T)[:S]),
        "ka": striped8(np.random.randint(0, G, (8, H))),
        "kb": striped8(np.random.randint(0, G, (8, H))),
        "n1": striped8(np.stack([np.random.permutation(S) for _ in range(8)])),
        "n2": striped8(np.stack([np.random.permutation(S) for _ in range(8)])),
        "n3": striped(perm[:S]),
        "n4": striped(perm[S:]),
        "n5": striped(np.random.permutation(S)),
    }


def reference(x_words, x_scales, d_words, d_scales, sl, th, gn, w1, offs, ka, kb, n1, n2, n3, n4, n5):
    d_ka = unpack_weight(d_words, d_scales)[np.arange(K)[:, None], runs(ka, K)]
    xq = unpack_weight(x_words, x_scales)[:, unstriped(offs)]
    d_kb = unpack_weight(d_words, d_scales)[np.arange(K)[:, None], runs(kb, K)]
    h = 0.0625 * (d_ka.T @ xq + d_kb.T @ xq)
    st = np.maximum(h, h[np.arange(H)[:, None], runs(n1, H)])
    sg = sigmoid(f64(sl) * (st[np.arange(H)[:, None], runs(n2, H)] - f64(th)))
    z = f64(gn) * (st * sg)
    h2 = mxq(f64(w1), 0, "e4m3").T @ mxq(z, 0, "e4m3")
    dn = np.minimum(h2, h2[:, unstriped(n5)])
    up = np.maximum(h2, h2[:, unstriped(n5)])
    ph = np.zeros((N, U))
    ph[:, unstriped(n3)] = up
    out = ph.copy()
    out[:, unstriped(n4)] = dn
    return out

@@ -1,0 +1,201 @@
+from contextlib import ExitStack
+
+import concourse.mybir as mybir
+from concourse.masks import make_identity
+
+K, T, S, N, G, H, U = 512, 1024, 256, 512, 2048, 512, 512
+FLOPS = 2 * (2 * K * H * S) + 2 * H * N * S
+
+F32 = mybir.dt.float32
+BF16 = mybir.dt.bfloat16
+I32 = mybir.dt.int32
+U32 = mybir.dt.uint32
+U16 = mybir.dt.uint16
+U8 = mybir.dt.uint8
+FP8X4 = mybir.dt.float8_e4m3fn_x4
+ALU = mybir.AluOpType
+ACT = mybir.ActivationFunctionType
+
+P = 128
+PACK = 4
+RUN = 8
+HALF = S // 2
+PER_COL = 16
+
+
+def tile_picked_aqlehhpagmx_none_p_kernel(
+    tc, x_words, x_scales, d_words, d_scales, sl, th, gn, w1, offs, ka, kb, n1, n2, n3, n4, n5, out
+):
+    nc = tc.nc
+    halves = [slice(0, HALF), slice(HALF, S)]
+    half_cols = [slice(0, HALF // PER_COL), slice(HALF // PER_COL, S // PER_COL)]
+
+    with ExitStack() as ctx:
+        keep = ctx.enter_context(tc.tile_pool(name="keep", bufs=1))
+        psum = ctx.enter_context(tc.psum_pool(name="psum", bufs=1))
+
+        def load_list(src, name):
+            tile = keep.tile(list(src.shape), U16, name=name)
+            nc.sync.dma_start(tile[:], src)
+            return tile
+
+        d_byte_table = keep.tile([P, G], U8)
+        x_byte_table = keep.tile([P, T], U8)
+        planes = keep.tile([P, 2 * H + S], U8, align_bytes=64)
+        nc.vector.memset(planes[:].bitcast(I32), 0)
+
+        ka_list = load_list(ka, "ka_list")
+        kb_list = load_list(kb, "kb_list")
+        nc.scalar.dma_start(d_byte_table[:].bitcast(I32), d_scales[0].bitcast(I32).unsqueeze(1).broadcast_to([P // RUN, RUN, G // 4]))
+        offs_list = load_list(offs, "offs_list")
+        nc.scalar.dma_start(x_byte_table[:].bitcast(I32), x_scales[0].bitcast(I32).unsqueeze(1).broadcast_to([P // RUN, RUN, T // 4]))
+        d_word_table = keep.tile([P, G], I32)
+        nc.sync.dma_start(d_word_table[:], d_words[0].rearrange("p c r -> p (c r)").bitcast(I32))
+        n1_list = load_list(n1, "n1_list")
+        n2_list = load_list(n2, "n2_list")
+        n5_list = load_list(n5, "n5_list")
+        n3_list = load_list(n3, "n3_list")
+        n4_list = load_list(n4, "n4_list")
+        w_raw = keep.tile([P, PACK, N], F32)
+        w_rows = w1.rearrange("(b t r) m -> t b r m", t=PACK, r=RUN)
+        for t in range(PACK):
+            nc.sync.dma_start(w_raw[:, t, :], w_rows[t])
+        x_word_table = keep.tile([P, T], I32)
+        nc.sync.dma_start(x_word_table[:], x_words[0].rearrange("p c r -> p (c r)").bitcast(I32))
+
+        rows_in = keep.tile([P, P], F32)
+        identity = keep.tile([P, P], F32)
+        nc.gpsimd.memset(rows_in[:], 0.0)
+        for v, src in enumerate((sl, th, gn)):
+            nc.gpsimd.dma_start(
+                rows_in[PACK * v : PACK * (v + 1), :].rearrange("t (b r) -> t b r", r=RUN),
+                src.rearrange("(b t r) o -> t b (r o)", t=PACK, r=RUN),
+            )
+        make_identity(nc, identity[:])
+        rows_acc = psum.tile([P, P], F32, tag="bank7")
+        nc.tensor.transpose(rows_acc[:], rows_in[:], identity[:])
+        per_row = keep.tile([P, 3 * PACK], F32)
+        nc.scalar.copy(per_row[:], rows_acc[:, 0 : 3 * PACK])
+        slope, thresh, gain = (per_row[:, PACK * v : PACK * (v + 1)] for v in range(3))
+        slope_thresh = keep.tile([P, PACK], F32)
+        bias = keep.tile([P, PACK], F32)
+        nc.gpsimd.tensor_tensor(slope_thresh[:], slope, thresh, ALU.mult)
+        nc.gpsimd.tensor_scalar(bias[:], slope_thresh[:], -1.0, 0.0, ALU.mult, ALU.add)
+
+        d_bytes = keep.tile([P, 2 * H], U8)
+        x_bytes = keep.tile([P, S], U8)
+        nc.vector.tensor_copy(d_bytes[:, 0:H], d_byte_table[:].indirect(ka_list[:]))
+        nc.vector.tensor_copy(d_bytes[:, H : 2 * H], d_byte_table[:].indirect(kb_list[:]))
+        nc.vector.tensor_copy(x_bytes[:], x_byte_table[:].indirect(offs_list[:]))
+        staged = keep.tile([P, 2 * H + S], U8)
+        nc.vector.tensor_copy(
+            staged[:, 0 : 2 * H].bitcast(I32).rearrange("p (l t b w) -> p l t b w", l=2, t=PACK, w=RUN // 4),
+            d_bytes[:].bitcast(I32).rearrange("p (l b t w) -> p l t b w", l=2, t=PACK, w=RUN // 4),
+        )
+        nc.vector.tensor_copy(staged[:, 2 * H :].bitcast(I32), x_bytes[:].bitcast(I32))
+        for a in range(4):
+            nc.sync.dma_start(planes[a:P:32, :].bitcast(I32), staged[RUN * a : P : 32, :].bitcast(I32))
+
+        d_codes = []
+        picked = []
+        for name, lst in (("a", ka_list), ("b", kb_list)):
+            tile = keep.tile([P, H], U32, name="picked_" + name)
+            nc.vector.tensor_copy(tile[:], d_word_table[:].bitcast(U32).indirect(lst[:]))
+            picked.append(tile)
+        x_codes = keep.tile([P, S], U32, align_bytes=64)
+        nc.vector.tensor_copy(x_codes[:], x_word_table[:].bitcast(U32).indirect(offs_list[:]))
+        for name, tile in zip("ab", picked):
+            dealt = keep.tile([P, H], I32, name="dealt_" + name, align_bytes=64)
+            nc.vector.tensor_copy(
+                dealt[:].rearrange("p (t b r) -> p t b r", t=PACK, r=RUN),
+                tile[:].bitcast(I32).rearrange("p (b t r) -> p t b r", t=PACK, r=RUN),
+            )
+            d_codes.append(dealt)
+
+        w_grouped = keep.tile([P, N, PACK], BF16, align_bytes=64)
+        w_codes = keep.tile([P, N], U32, align_bytes=64)
+        w_scales = keep.tile([P, N], U8, align_bytes=64)
+        for u in range(N // P):
+            cols = slice(u * P, (u + 1) * P)
+            nc.scalar.copy(
+                w_grouped[:, cols, :].rearrange("p (c i) t -> p c t i", i=4),
+                w_raw[:, :, cols].rearrange("p t (c i) -> p c t i", i=4),
+            )
+
+        h = []
+        for t in range(PACK):
+            acc = psum.tile([P, S], F32, name="h_acc%d" % t)
+            for l in range(2):
+                nc.tensor.matmul_mx(
+                    out=acc[:],
+                    lhsT=d_codes[l][:, t * P : (t + 1) * P].bitcast(FP8X4),
+                    lhsT_scale=planes[:, l * H + t * P : l * H + (t + 1) * P],
+                    rhs=x_codes[:].bitcast(FP8X4),
+                    rhs_scale=planes[:, 2 * H :],
+                    start=(l == 0),
+                    stop=(l == 1),
+                )
+            h_t = keep.tile([P, S], F32, name="h%d" % t)
+            nc.vector.tensor_scalar(h_t[:], acc[:], 0.0625, None, ALU.mult)
+            h.append(h_t)
+
+        st = []
+        for t in range(PACK):
+            h_at = keep.tile([P, S], F32, name="h_at%d" % t)
+            for half, cols in zip(halves, half_cols):
+                nc.scalar.activation(h_at[:, half], h[t][:].indirect(n1_list[:, cols]), ACT.Copy)
+            st_t = keep.tile([P, S], F32, name="st%d" % t)
+            nc.vector.tensor_tensor(st_t[:], h[t][:], h_at[:], ALU.max)
+            st.append(st_t)
+            cols = slice(t * P, (t + 1) * P)
+            nc.vector.quantize_mx(
+                out=w_codes[:, cols].bitcast(FP8X4),
+                scales=w_scales[:, cols],
+                in_=w_grouped[:, cols, :].rearrange("p c t -> p (c t)"),
+            )
+
+        h2_acc = [psum.tile([P, S], F32, name="h2_acc%d" % u, tag="bank%d" % (4 + u)) for u in range(N // P)]
+        for q, (half, cols) in enumerate(zip(halves, half_cols)):
+            z = keep.tile([P, PACK, HALF], BF16, name="z%d" % q)
+            for t in range(PACK):
+                sg = keep.tile([P, HALF], F32, name="sg%d_%d" % (q, t))
+                nc.scalar.activation(
+                    sg[:], st[t][:].indirect(n2_list[:, cols]), ACT.Sigmoid,
+                    bias=bias[:, t : t + 1], scale=slope[:, t : t + 1],
+                )
+                nc.vector.scalar_tensor_tensor(z[:, t, :], st[t][:, half], gain[:, t : t + 1], sg[:], ALU.mult, ALU.mult)
+            z_grouped = keep.tile([P, HALF, PACK], BF16, name="z_grouped%d" % q, align_bytes=64)
+            nc.vector.tensor_copy(
+                z_grouped[:].rearrange("p (c i) t -> p c t i", i=4),
+                z[:].rearrange("p t (c i) -> p c t i", i=4),
+            )
+            z_codes = keep.tile([P, HALF], U32, name="z_codes%d" % q, align_bytes=64)
+            z_scales = keep.tile([P, HALF], U8, name="z_scales%d" % q, align_bytes=64)
+            nc.vector.quantize_mx(
+                out=z_codes[:].bitcast(FP8X4), scales=z_scales[:], in_=z_grouped[:].rearrange("p c t -> p (c t)")
+            )
+            for u in range(N // P):
+                nc.tensor.matmul_mx(
+                    out=h2_acc[u][:, half],
+                    lhsT=w_codes[:, u * P : (u + 1) * P].bitcast(FP8X4),
+                    lhsT_scale=w_scales[:, u * P : (u + 1) * P],
+                    rhs=z_codes[:].bitcast(FP8X4),
+                    rhs_scale=z_scales[:],
+                    start=True,
+                    stop=True,
+                )
+
+        for u in range(N // P):
+            h2 = keep.tile([P, S], F32, name="h2_%d" % u)
+            nc.vector.tensor_copy(h2[:], h2_acc[u][:])
+            h2_at = keep.tile([P, S], F32, name="h2_at%d" % u)
+            for half, cols in zip(halves, half_cols):
+                nc.scalar.activation(h2_at[:, half], h2[:].indirect(n5_list[:, cols]), ACT.Copy)
+            up = keep.tile([P, S], F32, name="up%d" % u)
+            dn = keep.tile([P, S], F32, name="dn%d" % u)
+            nc.vector.tensor_tensor(up[:], h2[:], h2_at[:], ALU.max)
+            nc.vector.tensor_tensor(dn[:], h2[:], h2_at[:], ALU.min)
+            page = keep.tile([P, U], F32, name="page%d" % u)
+            nc.scalar.activation(page[:].indirect(n3_list[:]), up[:], ACT.Copy)
+            nc.scalar.activation(page[:].indirect(n4_list[:]), dn[:], ACT.Copy)
+            nc.sync.dma_start(out[u * P : (u + 1) * P, :], page[:])

@@ -72,6 +72,8 @@ def tile_picked_aqlehhpagmx_none_p_kernel(
                 src.rearrange("(b t r) o -> t b (r o)", t=PACK, r=RUN),
             )
         make_identity(nc, identity[:])
+        warm = keep.tile([P, 1], F32)
+        nc.scalar.activation(warm[:], identity[:, 0:1], ACT.Sigmoid)
         rows_acc = psum.tile([P, P], F32, tag="bank7")
         nc.tensor.transpose(rows_acc[:], rows_in[:], identity[:])
         per_row = keep.tile([P, 3 * PACK], F32)

@@ -21,6 +21,9 @@ PACK = 4
 RUN = 8
 HALF = S // 2
 PER_COL = 16
+EARLY = 2
+AT = (0, S, 2 * S, 4 * S)
+PIECES = ((0, 128), (128, 192), (192, 256))
 
 
 def tile_picked_aqlehhpagmx_none_p_kernel(
@@ -44,11 +47,15 @@ def tile_picked_aqlehhpagmx_none_p_kernel(
         planes = keep.tile([P, 2 * H + S], U8, align_bytes=64)
         nc.vector.memset(planes[:].bitcast(I32), 0)
 
-        ka_list = load_list(ka, "ka_list")
-        kb_list = load_list(kb, "kb_list")
-        nc.scalar.dma_start(d_byte_table[:].bitcast(I32), d_scales[0].bitcast(I32).unsqueeze(1).broadcast_to([P // RUN, RUN, G // 4]))
+        h_tiles = [keep.tile([P, 2 * S], F32, name="h%d" % t, tag="h%d" % t) for t in range(PACK)]
+        h2_tiles = [keep.tile([P, S + PER_COL], F32, name="h2_%d" % u) for u in range(N // P)]
+        for tile in h_tiles + h2_tiles:
+            nc.vector.memset(tile[:, S:], 0.0)
         offs_list = load_list(offs, "offs_list")
         nc.scalar.dma_start(x_byte_table[:].bitcast(I32), x_scales[0].bitcast(I32).unsqueeze(1).broadcast_to([P // RUN, RUN, T // 4]))
+        ka_list = load_list(ka, "ka_list")
+        nc.scalar.dma_start(d_byte_table[:].bitcast(I32), d_scales[0].bitcast(I32).unsqueeze(1).broadcast_to([P // RUN, RUN, G // 4]))
+        kb_list = load_list(kb, "kb_list")
         d_word_table = keep.tile([P, G], I32)
         nc.sync.dma_start(d_word_table[:], d_words[0].rearrange("p c r -> p (c r)").bitcast(I32))
         n1_list = load_list(n1, "n1_list")
@@ -65,13 +72,13 @@ def tile_picked_aqlehhpagmx_none_p_kernel(
 
         rows_in = keep.tile([P, P], F32)
         identity = keep.tile([P, P], F32)
+        make_identity(nc, identity[:])
         nc.gpsimd.memset(rows_in[:], 0.0)
         for v, src in enumerate((sl, th, gn)):
             nc.gpsimd.dma_start(
                 rows_in[PACK * v : PACK * (v + 1), :].rearrange("t (b r) -> t b r", r=RUN),
                 src.rearrange("(b t r) o -> t b (r o)", t=PACK, r=RUN),
             )
-        make_identity(nc, identity[:])
         warm = keep.tile([P, 1], F32)
         nc.scalar.activation(warm[:], identity[:, 0:1], ACT.Sigmoid)
         rows_acc = psum.tile([P, P], F32, tag="bank7")
@@ -86,9 +93,9 @@ def tile_picked_aqlehhpagmx_none_p_kernel(
 
         d_bytes = keep.tile([P, 2 * H], U8)
         x_bytes = keep.tile([P, S], U8)
+        nc.vector.tensor_copy(x_bytes[:], x_byte_table[:].indirect(offs_list[:]))
         nc.vector.tensor_copy(d_bytes[:, 0:H], d_byte_table[:].indirect(ka_list[:]))
         nc.vector.tensor_copy(d_bytes[:, H : 2 * H], d_byte_table[:].indirect(kb_list[:]))
-        nc.vector.tensor_copy(x_bytes[:], x_byte_table[:].indirect(offs_list[:]))
         staged = keep.tile([P, 2 * H + S], U8)
         nc.vector.tensor_copy(
             staged[:, 0 : 2 * H].bitcast(I32).rearrange("p (l t b w) -> p l t b w", l=2, t=PACK, w=RUN // 4),
@@ -98,105 +105,134 @@ def tile_picked_aqlehhpagmx_none_p_kernel(
         for a in range(4):
             nc.sync.dma_start(planes[a:P:32, :].bitcast(I32), staged[RUN * a : P : 32, :].bitcast(I32))
 
-        d_codes = []
-        picked = []
-        for name, lst in (("a", ka_list), ("b", kb_list)):
-            tile = keep.tile([P, H], U32, name="picked_" + name)
-            nc.vector.tensor_copy(tile[:], d_word_table[:].bitcast(U32).indirect(lst[:]))
-            picked.append(tile)
+        picked_a = keep.tile([P, H], U32)
+        picked_b = keep.tile([P, H], U32)
         x_codes = keep.tile([P, S], U32, align_bytes=64)
+        nc.vector.tensor_copy(picked_a[:], d_word_table[:].bitcast(U32).indirect(ka_list[:]))
+        nc.vector.tensor_copy(picked_b[:], d_word_table[:].bitcast(U32).indirect(kb_list[:]))
+        dealt_a = keep.tile([P, PACK, P], I32, align_bytes=64)
+        dealt_b = keep.tile([P, PACK, P], I32, align_bytes=64)
+        nc.vector.tensor_copy(
+            dealt_a[:].rearrange("p t (b r) -> p t b r", r=RUN),
+            picked_a[:].bitcast(I32).rearrange("p (b t r) -> p t b r", t=PACK, r=RUN),
+        )
+        nc.vector.tensor_copy(
+            dealt_b[:].rearrange("p t (b r) -> p t b r", r=RUN),
+            picked_b[:].bitcast(I32).rearrange("p (b t r) -> p t b r", t=PACK, r=RUN),
+        )
         nc.vector.tensor_copy(x_codes[:], x_word_table[:].bitcast(U32).indirect(offs_list[:]))
-        for name, tile in zip("ab", picked):
-            dealt = keep.tile([P, H], I32, name="dealt_" + name, align_bytes=64)
-            nc.vector.tensor_copy(
-                dealt[:].rearrange("p (t b r) -> p t b r", t=PACK, r=RUN),
-                tile[:].bitcast(I32).rearrange("p (b t r) -> p t b r", t=PACK, r=RUN),
-            )
-            d_codes.append(dealt)
 
-        w_grouped = keep.tile([P, N, PACK], BF16, align_bytes=64)
         w_codes = keep.tile([P, N], U32, align_bytes=64)
         w_scales = keep.tile([P, N], U8, align_bytes=64)
-        for u in range(N // P):
-            cols = slice(u * P, (u + 1) * P)
-            nc.scalar.copy(
-                w_grouped[:, cols, :].rearrange("p (c i) t -> p c t i", i=4),
-                w_raw[:, :, cols].rearrange("p t (c i) -> p c t i", i=4),
+
+        def group_w(u, copy, tag):
+            grouped = keep.tile([P, P, PACK], BF16, name="w_grouped%d" % u, tag=tag, align_bytes=64)
+            copy(
+                grouped[:].rearrange("p (c i) t -> p c t i", i=4),
+                w_raw[:, :, u * P : (u + 1) * P].rearrange("p t (c i) -> p c t i", i=4),
+            )
+            return grouped
+
+        def quantize_w(u, grouped):
+            nc.vector.quantize_mx(
+                out=w_codes[:, u * P : (u + 1) * P].bitcast(FP8X4),
+                scales=w_scales[:, u * P : (u + 1) * P],
+                in_=grouped[:].rearrange("p c t -> p (c t)"),
             )
 
-        h = []
+        w_early = [group_w(u, nc.scalar.copy, "w_early%d" % u) for u in range(EARLY)]
+
+        h_acc = [psum.tile([P, S], F32, name="h_acc%d" % t) for t in range(PACK)]
         for t in range(PACK):
-            acc = psum.tile([P, S], F32, name="h_acc%d" % t)
-            for l in range(2):
+            for l, dealt in enumerate((dealt_a, dealt_b)):
                 nc.tensor.matmul_mx(
-                    out=acc[:],
-                    lhsT=d_codes[l][:, t * P : (t + 1) * P].bitcast(FP8X4),
+                    out=h_acc[t][:],
+                    lhsT=dealt[:, t, :].bitcast(FP8X4),
                     lhsT_scale=planes[:, l * H + t * P : l * H + (t + 1) * P],
                     rhs=x_codes[:].bitcast(FP8X4),
                     rhs_scale=planes[:, 2 * H :],
                     start=(l == 0),
                     stop=(l == 1),
                 )
-            h_t = keep.tile([P, S], F32, name="h%d" % t)
-            nc.vector.tensor_scalar(h_t[:], acc[:], 0.0625, None, ALU.mult)
+        h = []
+        for t in range(PACK):
+            h_t = h_tiles[t]
+            if t == 0:
+                nc.scalar.activation(h_t[:, 0:S], h_acc[t][:], ACT.Copy, scale=0.0625)
+            else:
+                nc.vector.tensor_scalar(h_t[:, 0:S], h_acc[t][:], 0.0625, None, ALU.mult)
             h.append(h_t)
 
         st = []
+        fetched = keep.tile([P, 5 * S], F32)
+        gained = keep.tile([P, PACK, S], F32)
         for t in range(PACK):
-            h_at = keep.tile([P, S], F32, name="h_at%d" % t)
-            for half, cols in zip(halves, half_cols):
-                nc.scalar.activation(h_at[:, half], h[t][:].indirect(n1_list[:, cols]), ACT.Copy)
-            st_t = keep.tile([P, S], F32, name="st%d" % t)
-            nc.vector.tensor_tensor(st_t[:], h[t][:], h_at[:], ALU.max)
+            h_at = fetched[:, AT[t] : AT[t] + S]
+            nc.scalar.activation(h_at, h[t][:].indirect(n1_list[:]), ACT.Copy)
+            st_t = keep.tile([P, S], F32, name="st%d" % t, tag="st%d" % t, align_bytes=64)
+            nc.vector.tensor_tensor(st_t[:], h[t][:, 0:S], h_at, ALU.max)
             st.append(st_t)
-            cols = slice(t * P, (t + 1) * P)
-            nc.vector.quantize_mx(
-                out=w_codes[:, cols].bitcast(FP8X4),
-                scales=w_scales[:, cols],
-                in_=w_grouped[:, cols, :].rearrange("p c t -> p (c t)"),
-            )
+            nc.vector.tensor_scalar(gained[:, t, :], st_t[:], gain[:, t : t + 1], None, ALU.mult)
+        for u in range(EARLY):
+            quantize_w(u, w_early[u])
 
         h2_acc = [psum.tile([P, S], F32, name="h2_acc%d" % u, tag="bank%d" % (4 + u)) for u in range(N // P)]
-        for q, (half, cols) in enumerate(zip(halves, half_cols)):
-            z = keep.tile([P, PACK, HALF], BF16, name="z%d" % q)
+        h2 = h2_tiles
+        z_codes = keep.tile([P, S], U32, align_bytes=64)
+        z_scales = keep.tile([P, S], U8, align_bytes=64)
+
+        def second_product(u, part):
+            nc.tensor.matmul_mx(
+                out=h2_acc[u][:, part],
+                lhsT=w_codes[:, u * P : (u + 1) * P].bitcast(FP8X4),
+                lhsT_scale=w_scales[:, u * P : (u + 1) * P],
+                rhs=z_codes[:, part].bitcast(FP8X4),
+                rhs_scale=z_scales[:, part],
+                start=True,
+                stop=True,
+            )
+
+        for q, (lo, hi) in enumerate(PIECES):
+            part = slice(lo, hi)
+            if q == 0:
+                sg = fetched[:, AT[2] : AT[2] + PACK * (hi - lo)].rearrange("p (t j) -> p t j", t=PACK)
+            elif q == 1:
+                sg = fetched[:, AT[3] : AT[3] + PACK * (hi - lo)].rearrange("p (t j) -> p t j", t=PACK)
+            else:
+                sg_last = keep.tile([P, PACK, hi - lo], F32, tag="h3")
+                sg = sg_last[:]
             for t in range(PACK):
-                sg = keep.tile([P, HALF], F32, name="sg%d_%d" % (q, t))
                 nc.scalar.activation(
-                    sg[:], st[t][:].indirect(n2_list[:, cols]), ACT.Sigmoid,
+                    sg[:, t, :], st[t][:].indirect(n2_list[:, lo // PER_COL : hi // PER_COL]), ACT.Sigmoid,
                     bias=bias[:, t : t + 1], scale=slope[:, t : t + 1],
                 )
-                nc.vector.scalar_tensor_tensor(z[:, t, :], st[t][:, half], gain[:, t : t + 1], sg[:], ALU.mult, ALU.mult)
-            z_grouped = keep.tile([P, HALF, PACK], BF16, name="z_grouped%d" % q, align_bytes=64)
-            nc.vector.tensor_copy(
-                z_grouped[:].rearrange("p (c i) t -> p c t i", i=4),
-                z[:].rearrange("p t (c i) -> p c t i", i=4),
+            z = keep.tile([P, hi - lo, PACK], BF16, name="z%d" % q, align_bytes=64)
+            nc.vector.tensor_tensor(
+                z[:].rearrange("p (c i) t -> p c t i", i=4),
+                gained[:, :, part].rearrange("p t (c i) -> p c t i", i=4),
+                sg.rearrange("p t (c i) -> p c t i", i=4),
+                ALU.mult,
             )
-            z_codes = keep.tile([P, HALF], U32, name="z_codes%d" % q, align_bytes=64)
-            z_scales = keep.tile([P, HALF], U8, name="z_scales%d" % q, align_bytes=64)
             nc.vector.quantize_mx(
-                out=z_codes[:].bitcast(FP8X4), scales=z_scales[:], in_=z_grouped[:].rearrange("p c t -> p (c t)")
+                out=z_codes[:, part].bitcast(FP8X4), scales=z_scales[:, part], in_=z[:].rearrange("p c t -> p (c t)")
             )
-            for u in range(N // P):
-                nc.tensor.matmul_mx(
-                    out=h2_acc[u][:, half],
-                    lhsT=w_codes[:, u * P : (u + 1) * P].bitcast(FP8X4),
-                    lhsT_scale=w_scales[:, u * P : (u + 1) * P],
-                    rhs=z_codes[:].bitcast(FP8X4),
-                    rhs_scale=z_scales[:],
-                    start=True,
-                    stop=True,
-                )
+            if hi == S:
+                w_late = [group_w(u, nc.scalar.copy, "st%d" % u) for u in range(EARLY, N // P)]
+            second_product(0, part)
+        nc.scalar.copy(h2[0][:, 0:S], h2_acc[0][:])
 
         for u in range(N // P):
-            h2 = keep.tile([P, S], F32, name="h2_%d" % u)
-            nc.vector.tensor_copy(h2[:], h2_acc[u][:])
+            if u >= EARLY:
+                quantize_w(u, w_late[u - EARLY])
+            if u > 0:
+                second_product(u, slice(0, S))
+                nc.vector.tensor_copy(h2[u][:, 0:S], h2_acc[u][:])
             h2_at = keep.tile([P, S], F32, name="h2_at%d" % u)
-            for half, cols in zip(halves, half_cols):
-                nc.scalar.activation(h2_at[:, half], h2[:].indirect(n5_list[:, cols]), ACT.Copy)
+            nc.scalar.activation(h2_at[:], h2[u][:].indirect(n5_list[:]), ACT.Copy)
             up = keep.tile([P, S], F32, name="up%d" % u)
             dn = keep.tile([P, S], F32, name="dn%d" % u)
-            nc.vector.tensor_tensor(up[:], h2[:], h2_at[:], ALU.max)
-            nc.vector.tensor_tensor(dn[:], h2[:], h2_at[:], ALU.min)
+            nc.vector.tensor_tensor(up[:], h2[u][:, 0:S], h2_at[:], ALU.max)
+            nc.vector.tensor_tensor(dn[:], h2[u][:, 0:S], h2_at[:], ALU.min)
             page = keep.tile([P, U], F32, name="page%d" % u)
             nc.scalar.activation(page[:].indirect(n3_list[:]), up[:], ACT.Copy)
             nc.scalar.activation(page[:].indirect(n4_list[:]), dn[:], ACT.Copy)

@@ -56,19 +56,20 @@ def tile_picked_aqlehhpagmx_none_p_kernel(
         ka_list = load_list(ka, "ka_list")
         nc.scalar.dma_start(d_byte_table[:].bitcast(I32), d_scales[0].bitcast(I32).unsqueeze(1).broadcast_to([P // RUN, RUN, G // 4]))
         kb_list = load_list(kb, "kb_list")
-        d_word_table = keep.tile([P, G], I32)
-        nc.sync.dma_start(d_word_table[:], d_words[0].rearrange("p c r -> p (c r)").bitcast(I32))
         n1_list = load_list(n1, "n1_list")
         n2_list = load_list(n2, "n2_list")
+        d_word_table = keep.tile([P, G], I32, tag="d_words")
+        nc.sync.dma_start(d_word_table[:], d_words[0].rearrange("p c r -> p (c r)").bitcast(I32))
         n5_list = load_list(n5, "n5_list")
         n3_list = load_list(n3, "n3_list")
         n4_list = load_list(n4, "n4_list")
-        w_raw = keep.tile([P, PACK, N], F32)
         w_rows = w1.rearrange("(b t r) m -> t b r m", t=PACK, r=RUN)
-        for t in range(PACK):
-            nc.sync.dma_start(w_raw[:, t, :], w_rows[t])
-        x_word_table = keep.tile([P, T], I32)
+        w_raw_early = keep.tile([P, PACK, EARLY * P], F32)
+        nc.sync.dma_start(w_raw_early[:, 0, :], w_rows[0, :, :, 0 : EARLY * P])
+        x_word_table = keep.tile([P, T], I32, tag="x_words", align_bytes=64)
         nc.sync.dma_start(x_word_table[:], x_words[0].rearrange("p c r -> p (c r)").bitcast(I32))
+        for t in range(1, PACK):
+            nc.sync.dma_start(w_raw_early[:, t, :], w_rows[t, :, :, 0 : EARLY * P])
 
         rows_in = keep.tile([P, P], F32)
         identity = keep.tile([P, P], F32)
@@ -80,16 +81,9 @@ def tile_picked_aqlehhpagmx_none_p_kernel(
                 src.rearrange("(b t r) o -> t b (r o)", t=PACK, r=RUN),
             )
         warm = keep.tile([P, 1], F32)
-        nc.scalar.activation(warm[:], identity[:, 0:1], ACT.Sigmoid)
+        nc.scalar.activation(warm[:], h_tiles[0][:, S : S + 1], ACT.Sigmoid)
         rows_acc = psum.tile([P, P], F32, tag="bank7")
         nc.tensor.transpose(rows_acc[:], rows_in[:], identity[:])
-        per_row = keep.tile([P, 3 * PACK], F32)
-        nc.scalar.copy(per_row[:], rows_acc[:, 0 : 3 * PACK])
-        slope, thresh, gain = (per_row[:, PACK * v : PACK * (v + 1)] for v in range(3))
-        slope_thresh = keep.tile([P, PACK], F32)
-        bias = keep.tile([P, PACK], F32)
-        nc.gpsimd.tensor_tensor(slope_thresh[:], slope, thresh, ALU.mult)
-        nc.gpsimd.tensor_scalar(bias[:], slope_thresh[:], -1.0, 0.0, ALU.mult, ALU.add)
 
         d_bytes = keep.tile([P, 2 * H], U8)
         x_bytes = keep.tile([P, S], U8)
@@ -106,30 +100,36 @@ def tile_picked_aqlehhpagmx_none_p_kernel(
             nc.sync.dma_start(planes[a:P:32, :].bitcast(I32), staged[RUN * a : P : 32, :].bitcast(I32))
 
         picked_a = keep.tile([P, H], U32)
-        picked_b = keep.tile([P, H], U32)
         x_codes = keep.tile([P, S], U32, align_bytes=64)
         nc.vector.tensor_copy(picked_a[:], d_word_table[:].bitcast(U32).indirect(ka_list[:]))
+        nc.vector.tensor_copy(x_codes[:], x_word_table[:].bitcast(U32).indirect(offs_list[:]))
+        picked_b = keep.tile([P, H], U32, tag="x_words", align_bytes=64)
         nc.vector.tensor_copy(picked_b[:], d_word_table[:].bitcast(U32).indirect(kb_list[:]))
+        w_raw_late = keep.tile([P, PACK, N - EARLY * P], F32, tag="d_words")
+        for t in range(PACK):
+            nc.sync.dma_start(w_raw_late[:, t, :], w_rows[t, :, :, EARLY * P :])
+        w_raw = [w_raw_early[:, :, u * P : (u + 1) * P] for u in range(EARLY)]
+        w_raw = w_raw + [w_raw_late[:, :, u * P : (u + 1) * P] for u in range(N // P - EARLY)]
         dealt_a = keep.tile([P, PACK, P], I32, align_bytes=64)
         dealt_b = keep.tile([P, PACK, P], I32, align_bytes=64)
         nc.vector.tensor_copy(
             dealt_a[:].rearrange("p t (b r) -> p t b r", r=RUN),
             picked_a[:].bitcast(I32).rearrange("p (b t r) -> p t b r", t=PACK, r=RUN),
         )
-        nc.vector.tensor_copy(
-            dealt_b[:].rearrange("p t (b r) -> p t b r", r=RUN),
-            picked_b[:].bitcast(I32).rearrange("p (b t r) -> p t b r", t=PACK, r=RUN),
-        )
-        nc.vector.tensor_copy(x_codes[:], x_word_table[:].bitcast(U32).indirect(offs_list[:]))
+        for t in range(PACK):
+            nc.vector.tensor_copy(
+                dealt_b[:, t, :].rearrange("p (b r) -> p b r", r=RUN),
+                picked_b[:].bitcast(I32).rearrange("p (b t r) -> p t b r", t=PACK, r=RUN)[:, t],
+            )
 
-        w_codes = keep.tile([P, N], U32, align_bytes=64)
+        w_codes = keep.tile([P, N], U32, tag="x_words", align_bytes=64)
         w_scales = keep.tile([P, N], U8, align_bytes=64)
 
         def group_w(u, copy, tag):
             grouped = keep.tile([P, P, PACK], BF16, name="w_grouped%d" % u, tag=tag, align_bytes=64)
             copy(
                 grouped[:].rearrange("p (c i) t -> p c t i", i=4),
-                w_raw[:, :, u * P : (u + 1) * P].rearrange("p t (c i) -> p c t i", i=4),
+                w_raw[u].rearrange("p t (c i) -> p c t i", i=4),
             )
             return grouped
 
@@ -142,9 +142,17 @@ def tile_picked_aqlehhpagmx_none_p_kernel(
 
         w_early = [group_w(u, nc.scalar.copy, "w_early%d" % u) for u in range(EARLY)]
 
+        per_row = w_raw[EARLY - 1][:, 1, 0 : 3 * PACK]
+        nc.scalar.copy(per_row, rows_acc[:, 0 : 3 * PACK])
+        slope, thresh, gain = (per_row[:, PACK * v : PACK * (v + 1)] for v in range(3))
+        slope_thresh = keep.tile([P, PACK], F32)
+        bias = keep.tile([P, PACK], F32)
+        nc.gpsimd.tensor_tensor(slope_thresh[:], slope, thresh, ALU.mult)
+        nc.gpsimd.tensor_scalar(bias[:], slope_thresh[:], -1.0, 0.0, ALU.mult, ALU.add)
+
         h_acc = [psum.tile([P, S], F32, name="h_acc%d" % t) for t in range(PACK)]
-        for t in range(PACK):
-            for l, dealt in enumerate((dealt_a, dealt_b)):
+        for l, dealt in enumerate((dealt_a, dealt_b)):
+            for t in range(PACK):
                 nc.tensor.matmul_mx(
                     out=h_acc[t][:],
                     lhsT=dealt[:, t, :].bitcast(FP8X4),
@@ -167,7 +175,7 @@ def tile_picked_aqlehhpagmx_none_p_kernel(
         fetched = keep.tile([P, 5 * S], F32)
         gained = keep.tile([P, PACK, S], F32)
         for t in range(PACK):
-            h_at = fetched[:, AT[t] : AT[t] + S]
+            h_at = w_raw_early[:, 0, :] if t == 0 else fetched[:, AT[t] : AT[t] + S]
             nc.scalar.activation(h_at, h[t][:].indirect(n1_list[:]), ACT.Copy)
             st_t = keep.tile([P, S], F32, name="st%d" % t, tag="st%d" % t, align_bytes=64)
             nc.vector.tensor_tensor(st_t[:], h[t][:, 0:S], h_at, ALU.max)

from contextlib import ExitStack

import concourse.mybir as mybir
from concourse.masks import make_identity

K, T, S, N, G, H, U = 512, 1024, 256, 512, 2048, 512, 512
FLOPS = 2 * (2 * K * H * S) + 2 * H * N * S

F32 = mybir.dt.float32
BF16 = mybir.dt.bfloat16
I32 = mybir.dt.int32
U32 = mybir.dt.uint32
U16 = mybir.dt.uint16
U8 = mybir.dt.uint8
FP8X4 = mybir.dt.float8_e4m3fn_x4
ALU = mybir.AluOpType
ACT = mybir.ActivationFunctionType

P = 128
PACK = 4
RUN = 8
HALF = S // 2
PER_COL = 16
EARLY = 2
AT = (0, S, 2 * S, 4 * S)
PIECES = ((0, 128), (128, 192), (192, 256))


def tile_picked_aqlehhpagmx_none_p_kernel(
    tc, x_words, x_scales, d_words, d_scales, sl, th, gn, w1, offs, ka, kb, n1, n2, n3, n4, n5, out
):
    nc = tc.nc
    halves = [slice(0, HALF), slice(HALF, S)]
    half_cols = [slice(0, HALF // PER_COL), slice(HALF // PER_COL, S // PER_COL)]

    with ExitStack() as ctx:
        keep = ctx.enter_context(tc.tile_pool(name="keep", bufs=1))
        psum = ctx.enter_context(tc.psum_pool(name="psum", bufs=1))

        def load_list(src, name):
            tile = keep.tile(list(src.shape), U16, name=name)
            nc.sync.dma_start(tile[:], src)
            return tile

        d_byte_table = keep.tile([P, G], U8)
        x_byte_table = keep.tile([P, T], U8)
        planes = keep.tile([P, 2 * H + S], U8, align_bytes=64)
        nc.vector.memset(planes[:].bitcast(I32), 0)

        h_tiles = [keep.tile([P, 2 * S], F32, name="h%d" % t, tag="h%d" % t) for t in range(PACK)]
        h2_tiles = [keep.tile([P, S + PER_COL], F32, name="h2_%d" % u) for u in range(N // P)]
        for tile in h_tiles + h2_tiles:
            nc.vector.memset(tile[:, S:], 0.0)
        offs_list = load_list(offs, "offs_list")
        nc.scalar.dma_start(x_byte_table[:].bitcast(I32), x_scales[0].bitcast(I32).unsqueeze(1).broadcast_to([P // RUN, RUN, T // 4]))
        ka_list = load_list(ka, "ka_list")
        nc.scalar.dma_start(d_byte_table[:].bitcast(I32), d_scales[0].bitcast(I32).unsqueeze(1).broadcast_to([P // RUN, RUN, G // 4]))
        kb_list = load_list(kb, "kb_list")
        n1_list = load_list(n1, "n1_list")
        n2_list = load_list(n2, "n2_list")
        d_word_table = keep.tile([P, G], I32, tag="d_words")
        nc.sync.dma_start(d_word_table[:], d_words[0].rearrange("p c r -> p (c r)").bitcast(I32))
        n5_list = load_list(n5, "n5_list")
        n3_list = load_list(n3, "n3_list")
        n4_list = load_list(n4, "n4_list")
        w_rows = w1.rearrange("(b t r) m -> t b r m", t=PACK, r=RUN)
        w_raw_early = keep.tile([P, PACK, EARLY * P], F32)
        nc.sync.dma_start(w_raw_early[:, 0, :], w_rows[0, :, :, 0 : EARLY * P])
        x_word_table = keep.tile([P, T], I32, tag="x_words", align_bytes=64)
        nc.sync.dma_start(x_word_table[:], x_words[0].rearrange("p c r -> p (c r)").bitcast(I32))
        for t in range(1, PACK):
            nc.sync.dma_start(w_raw_early[:, t, :], w_rows[t, :, :, 0 : EARLY * P])

        rows_in = keep.tile([P, P], F32)
        identity = keep.tile([P, P], F32)
        make_identity(nc, identity[:])
        nc.gpsimd.memset(rows_in[:], 0.0)
        for v, src in enumerate((sl, th, gn)):
            nc.gpsimd.dma_start(
                rows_in[PACK * v : PACK * (v + 1), :].rearrange("t (b r) -> t b r", r=RUN),
                src.rearrange("(b t r) o -> t b (r o)", t=PACK, r=RUN),
            )
        warm = keep.tile([P, 1], F32)
        nc.scalar.activation(warm[:], h_tiles[0][:, S : S + 1], ACT.Sigmoid)
        rows_acc = psum.tile([P, P], F32, tag="bank7")
        nc.tensor.transpose(rows_acc[:], rows_in[:], identity[:])

        d_bytes = keep.tile([P, 2 * H], U8)
        x_bytes = keep.tile([P, S], U8)
        nc.vector.tensor_copy(x_bytes[:], x_byte_table[:].indirect(offs_list[:]))
        nc.vector.tensor_copy(d_bytes[:, 0:H], d_byte_table[:].indirect(ka_list[:]))
        nc.vector.tensor_copy(d_bytes[:, H : 2 * H], d_byte_table[:].indirect(kb_list[:]))
        staged = keep.tile([P, 2 * H + S], U8)
        nc.vector.tensor_copy(
            staged[:, 0 : 2 * H].bitcast(I32).rearrange("p (l t b w) -> p l t b w", l=2, t=PACK, w=RUN // 4),
            d_bytes[:].bitcast(I32).rearrange("p (l b t w) -> p l t b w", l=2, t=PACK, w=RUN // 4),
        )
        nc.vector.tensor_copy(staged[:, 2 * H :].bitcast(I32), x_bytes[:].bitcast(I32))
        for a in range(4):
            nc.sync.dma_start(planes[a:P:32, :].bitcast(I32), staged[RUN * a : P : 32, :].bitcast(I32))

        picked_a = keep.tile([P, H], U32)
        x_codes = keep.tile([P, S], U32, align_bytes=64)
        nc.vector.tensor_copy(picked_a[:], d_word_table[:].bitcast(U32).indirect(ka_list[:]))
        nc.vector.tensor_copy(x_codes[:], x_word_table[:].bitcast(U32).indirect(offs_list[:]))
        picked_b = keep.tile([P, H], U32, tag="x_words", align_bytes=64)
        nc.vector.tensor_copy(picked_b[:], d_word_table[:].bitcast(U32).indirect(kb_list[:]))
        w_raw_late = keep.tile([P, PACK, N - EARLY * P], F32, tag="d_words")
        for t in range(PACK):
            nc.sync.dma_start(w_raw_late[:, t, :], w_rows[t, :, :, EARLY * P :])
        w_raw = [w_raw_early[:, :, u * P : (u + 1) * P] for u in range(EARLY)]
        w_raw = w_raw + [w_raw_late[:, :, u * P : (u + 1) * P] for u in range(N // P - EARLY)]
        dealt_a = keep.tile([P, PACK, P], I32, align_bytes=64)
        dealt_b = keep.tile([P, PACK, P], I32, align_bytes=64)
        nc.vector.tensor_copy(
            dealt_a[:].rearrange("p t (b r) -> p t b r", r=RUN),
            picked_a[:].bitcast(I32).rearrange("p (b t r) -> p t b r", t=PACK, r=RUN),
        )
        for t in range(PACK):
            nc.vector.tensor_copy(
                dealt_b[:, t, :].rearrange("p (b r) -> p b r", r=RUN),
                picked_b[:].bitcast(I32).rearrange("p (b t r) -> p t b r", t=PACK, r=RUN)[:, t],
            )

        w_codes = keep.tile([P, N], U32, tag="x_words", align_bytes=64)
        w_scales = keep.tile([P, N], U8, align_bytes=64)

        def group_w(u, copy, tag):
            grouped = keep.tile([P, P, PACK], BF16, name="w_grouped%d" % u, tag=tag, align_bytes=64)
            copy(
                grouped[:].rearrange("p (c i) t -> p c t i", i=4),
                w_raw[u].rearrange("p t (c i) -> p c t i", i=4),
            )
            return grouped

        def quantize_w(u, grouped):
            nc.vector.quantize_mx(
                out=w_codes[:, u * P : (u + 1) * P].bitcast(FP8X4),
                scales=w_scales[:, u * P : (u + 1) * P],
                in_=grouped[:].rearrange("p c t -> p (c t)"),
            )

        w_early = [group_w(u, nc.scalar.copy, "w_early%d" % u) for u in range(EARLY)]

        per_row = w_raw[EARLY - 1][:, 1, 0 : 3 * PACK]
        nc.scalar.copy(per_row, rows_acc[:, 0 : 3 * PACK])
        slope, thresh, gain = (per_row[:, PACK * v : PACK * (v + 1)] for v in range(3))
        slope_thresh = keep.tile([P, PACK], F32)
        bias = keep.tile([P, PACK], F32)
        nc.gpsimd.tensor_tensor(slope_thresh[:], slope, thresh, ALU.mult)
        nc.gpsimd.tensor_scalar(bias[:], slope_thresh[:], -1.0, 0.0, ALU.mult, ALU.add)

        h_acc = [psum.tile([P, S], F32, name="h_acc%d" % t) for t in range(PACK)]
        for l, dealt in enumerate((dealt_a, dealt_b)):
            for t in range(PACK):
                nc.tensor.matmul_mx(
                    out=h_acc[t][:],
                    lhsT=dealt[:, t, :].bitcast(FP8X4),
                    lhsT_scale=planes[:, l * H + t * P : l * H + (t + 1) * P],
                    rhs=x_codes[:].bitcast(FP8X4),
                    rhs_scale=planes[:, 2 * H :],
                    start=(l == 0),
                    stop=(l == 1),
                )
        h = []
        for t in range(PACK):
            h_t = h_tiles[t]
            if t == 0:
                nc.scalar.activation(h_t[:, 0:S], h_acc[t][:], ACT.Copy, scale=0.0625)
            else:
                nc.vector.tensor_scalar(h_t[:, 0:S], h_acc[t][:], 0.0625, None, ALU.mult)
            h.append(h_t)

        st = []
        fetched = keep.tile([P, 5 * S], F32)
        gained = keep.tile([P, PACK, S], F32)
        for t in range(PACK):
            h_at = w_raw_early[:, 0, :] if t == 0 else fetched[:, AT[t] : AT[t] + S]
            nc.scalar.activation(h_at, h[t][:].indirect(n1_list[:]), ACT.Copy)
            st_t = keep.tile([P, S], F32, name="st%d" % t, tag="st%d" % t, align_bytes=64)
            nc.vector.tensor_tensor(st_t[:], h[t][:, 0:S], h_at, ALU.max)
            st.append(st_t)
            nc.vector.tensor_scalar(gained[:, t, :], st_t[:], gain[:, t : t + 1], None, ALU.mult)
        for u in range(EARLY):
            quantize_w(u, w_early[u])

        h2_acc = [psum.tile([P, S], F32, name="h2_acc%d" % u, tag="bank%d" % (4 + u)) for u in range(N // P)]
        h2 = h2_tiles
        z_codes = keep.tile([P, S], U32, align_bytes=64)
        z_scales = keep.tile([P, S], U8, align_bytes=64)

        def second_product(u, part):
            nc.tensor.matmul_mx(
                out=h2_acc[u][:, part],
                lhsT=w_codes[:, u * P : (u + 1) * P].bitcast(FP8X4),
                lhsT_scale=w_scales[:, u * P : (u + 1) * P],
                rhs=z_codes[:, part].bitcast(FP8X4),
                rhs_scale=z_scales[:, part],
                start=True,
                stop=True,
            )

        for q, (lo, hi) in enumerate(PIECES):
            part = slice(lo, hi)
            if q == 0:
                sg = fetched[:, AT[2] : AT[2] + PACK * (hi - lo)].rearrange("p (t j) -> p t j", t=PACK)
            elif q == 1:
                sg = fetched[:, AT[3] : AT[3] + PACK * (hi - lo)].rearrange("p (t j) -> p t j", t=PACK)
            else:
                sg_last = keep.tile([P, PACK, hi - lo], F32, tag="h3")
                sg = sg_last[:]
            for t in range(PACK):
                nc.scalar.activation(
                    sg[:, t, :], st[t][:].indirect(n2_list[:, lo // PER_COL : hi // PER_COL]), ACT.Sigmoid,
                    bias=bias[:, t : t + 1], scale=slope[:, t : t + 1],
                )
            z = keep.tile([P, hi - lo, PACK], BF16, name="z%d" % q, align_bytes=64)
            nc.vector.tensor_tensor(
                z[:].rearrange("p (c i) t -> p c t i", i=4),
                gained[:, :, part].rearrange("p t (c i) -> p c t i", i=4),
                sg.rearrange("p t (c i) -> p c t i", i=4),
                ALU.mult,
            )
            nc.vector.quantize_mx(
                out=z_codes[:, part].bitcast(FP8X4), scales=z_scales[:, part], in_=z[:].rearrange("p c t -> p (c t)")
            )
            if hi == S:
                w_late = [group_w(u, nc.scalar.copy, "st%d" % u) for u in range(EARLY, N // P)]
            second_product(0, part)
        nc.scalar.copy(h2[0][:, 0:S], h2_acc[0][:])

        for u in range(N // P):
            if u >= EARLY:
                quantize_w(u, w_late[u - EARLY])
            if u > 0:
                second_product(u, slice(0, S))
                nc.vector.tensor_copy(h2[u][:, 0:S], h2_acc[u][:])
            h2_at = keep.tile([P, S], F32, name="h2_at%d" % u)
            nc.scalar.activation(h2_at[:], h2[u][:].indirect(n5_list[:]), ACT.Copy)
            up = keep.tile([P, S], F32, name="up%d" % u)
            dn = keep.tile([P, S], F32, name="dn%d" % u)
            nc.vector.tensor_tensor(up[:], h2[u][:, 0:S], h2_at[:], ALU.max)
            nc.vector.tensor_tensor(dn[:], h2[u][:, 0:S], h2_at[:], ALU.min)
            page = keep.tile([P, U], F32, name="page%d" % u)
            nc.scalar.activation(page[:].indirect(n3_list[:]), up[:], ACT.Copy)
            nc.scalar.activation(page[:].indirect(n4_list[:]), dn[:], ACT.Copy)
            nc.sync.dma_start(out[u * P : (u + 1) * P, :], page[:])
